import numpy as np
import ml_dtypes


def mxq(x, axis, fmt="e4m3"):
    dtype, down = {"e4m3": (ml_dtypes.float8_e4m3fn, 7), "e5m2": (ml_dtypes.float8_e5m2, 14)}[fmt]
    v = np.moveaxis(np.asarray(x, np.float32).astype(ml_dtypes.bfloat16).astype(np.float64), axis, -1)
    blocks = v.reshape(v.shape[:-1] + (-1, 32))
    amax = np.abs(blocks).max(-1, keepdims=True)
    byte = np.maximum(np.where(amax > 0, np.frexp(amax)[1] - 1 + 127, 0) - down, 1)
    scale = np.exp2(byte - 127.0)
    codes = (blocks / scale).astype(np.float32).astype(dtype).astype(np.float64)
    return np.moveaxis((codes * scale).reshape(v.shape), -1, axis)


WIDE = False


def mx_kscale(k):
    if not WIDE:
        return np.ones(k)
    levels = np.array([30, -30])
    if k % 512:
        return np.exp2(np.random.permutation(np.resize(levels, k // 32))).repeat(32)
    a = np.empty((k // 512, 16))
    for p in range(k // 512):
        a[p, :8] = np.random.permutation(np.resize(levels, 8))
        for g in range(8):
            far = levels[np.abs(levels - a[p, g]) >= 10]
            a[p, g + 8] = far[np.random.randint(len(far))]
    return np.exp2(a.ravel()).repeat(32)


def f64(x):
    return np.asarray(x).astype(np.float64)


def striped(idx):
    return np.tile(np.asarray(idx).reshape(-1, 16).T, (8, 1)).astype(np.uint16)


def unstriped(offs):
    return offs[:16].T.reshape(-1).astype(np.int64)


def sigmoid(v):
    return 1.0 / (1.0 + np.exp(-v))


K, N, T, J = 512, 512, 2048, 512


def setup_inputs():
    n = np.random.standard_normal
    idx = np.random.permutation(T)[:J]
    fj = mx_kscale(J)
    tj = np.ones(T)
    tj[idx] = fj
    return {
        "xt": (n((K, T)) * tj).astype(np.float32),
        "g": (n((N, T)) * np.exp(0.5 * n((1, T))) / tj).astype(np.float32),
        "mom": (1.0 * n((K, N))).astype(np.float32),
        "offs": striped(idx),
    }


def reference(xt, g, mom, offs):
    idx = unstriped(offs)
    xj = f64(xt)[:, idx].T
    gj = f64(g)[:, idx].T
    xjq = mxq(xj, 0, "e4m3")
    gjq = mxq(gj, 0, "e5m2")
    w0 = xjq.T @ gjq
    w = 0.04 * w0
    y = w * sigmoid(2.0 * w * f64(mom))
    return y

@@ -1,0 +1,124 @@
+from contextlib import ExitStack
+
+import concourse.mybir as mybir
+from concourse.masks import make_identity
+
+K, N, T, J = 512, 512, 2048, 512
+FLOPS = 2 * K * N * J
+
+F32 = mybir.dt.float32
+BF16 = mybir.dt.bfloat16
+U32 = mybir.dt.uint32
+U16 = mybir.dt.uint16
+U8 = mybir.dt.uint8
+E4M3 = mybir.dt.float8_e4m3fn_x4
+E5M2 = mybir.dt.float8_e5m2_x4
+MULT = mybir.AluOpType.mult
+SIGMOID = mybir.ActivationFunctionType.Sigmoid
+
+P = 128
+TILES = 4
+STEP = 0.04
+
+
+def tile_list_agreeing_update_kernel(tc, xt, g, mom, offs, out):
+    nc = tc.nc
+    with ExitStack() as ctx:
+        keep = ctx.enter_context(tc.tile_pool(name="keep", bufs=1))
+        ring = ctx.enter_context(tc.tile_pool(name="ring", bufs=3))
+        turn_psum = ctx.enter_context(tc.psum_pool(name="turn_psum", bufs=3))
+        acc_psum = ctx.enter_context(tc.psum_pool(name="acc_psum", bufs=4))
+
+        offsets = keep.tile([P, J // 16], U16, name="offsets")
+        g_rows = [keep.tile([P, T], F32, name="g_rows%d" % i) for i in range(TILES)]
+        x_rows = [keep.tile([P, T], F32, name="x_rows%d" % i) for i in range(TILES)]
+        mom_pair = [keep.tile([P, 2, N], F32, name="mom_pair%d" % h) for h in range(2)]
+        x_view = xt.rearrange("(p i) t -> p i t", i=TILES)
+        mom_view = mom.rearrange("(p i) n -> p i n", i=TILES)
+        out_view = out.rearrange("(p i) n -> p i n", i=TILES)
+
+        nc.sync.dma_start(out=g_rows[0][:], in_=g[0:P, :])
+        nc.sync.dma_start(offsets[:], offs)
+        for i in range(1, TILES):
+            nc.sync.dma_start(out=g_rows[i][:], in_=g[i * P:(i + 1) * P, :])
+        nc.sync.dma_start(out=x_rows[0][:], in_=x_view[:, 0, :])
+        nc.sync.dma_start(out=mom_pair[0][:], in_=mom_view[:, 0:2, :])
+        for i in range(1, TILES):
+            nc.sync.dma_start(out=x_rows[i][:], in_=x_view[:, i, :])
+        nc.sync.dma_start(out=mom_pair[1][:], in_=mom_view[:, 2:4, :])
+
+        ident = keep.tile([P, P], F32, name="ident")
+        make_identity(nc, ident[:])
+
+        g_codes = keep.tile([P, N], U32, name="g_codes", align_bytes=64)
+        g_scales = keep.tile([P, N], U8, name="g_scales", align_bytes=64)
+        x_codes = [keep.tile([P, P], U32, name="x_codes%d" % i, align_bytes=64) for i in range(TILES)]
+        x_scales = [keep.tile([P, P], U8, name="x_scales%d" % i, align_bytes=64) for i in range(TILES)]
+
+        def gather_and_turn(rows):
+            picked = ring.tile([P, J], BF16, name="picked", align_bytes=64)
+            nc.vector.tensor_copy(picked[:], rows[:].indirect(offsets[:]))
+            words = picked[:].bitcast(F32)
+            turned = turn_psum.tile([P, 2, P], F32, name="turned")
+            for u in range(2):
+                nc.tensor.transpose(turned[:, u, :], words[:, u:J // 2:2], ident[:])
+            grouped = ring.tile([P, 4 * P], BF16, name="grouped", align_bytes=64)
+            nc.scalar.copy(
+                out=grouped[:].bitcast(F32).rearrange("p (r u) -> p r u", u=2),
+                in_=turned[:].rearrange("p u r -> p r u"),
+            )
+            return grouped
+
+        def multiply(i, grouped):
+            nc.vector.quantize_mx(out=x_codes[i][:].bitcast(E4M3), scales=x_scales[i][:], in_=grouped[:])
+            acc = acc_psum.tile([P, N], F32, name="acc")
+            nc.tensor.matmul_mx(
+                out=acc[:],
+                lhsT=x_codes[i][:].bitcast(E4M3),
+                lhsT_scale=x_scales[i][:],
+                rhs=g_codes[:].bitcast(E5M2),
+                rhs_scale=g_scales[:],
+                start=True,
+                stop=True,
+            )
+            return acc
+
+        def agree(i, acc, cols):
+            width = cols.stop - cols.start
+            agreement = ring.tile([P, width], F32, name="agreement")
+            nc.vector.tensor_tensor(agreement[:], acc[:, cols], mom_pair[i // 2][:, i % 2, cols], MULT)
+            gate = ring.tile([P, width], F32, name="gate")
+            nc.scalar.activation(gate[:], agreement[:], SIGMOID, scale=2.0 * STEP)
+            return gate
+
+        def finish(i, acc, cols, gate):
+            width = cols.stop - cols.start
+            result = ring.tile([P, width], F32, name="result")
+            nc.vector.scalar_tensor_tensor(result[:], acc[:, cols], STEP, gate[:], MULT, MULT)
+            nc.sync.dma_start(out=out_view[:, i, cols], in_=result[:])
+
+        def quantize_g(i, grouped):
+            cols = slice(i * P, (i + 1) * P)
+            nc.vector.quantize_mx(out=g_codes[:, cols].bitcast(E5M2), scales=g_scales[:, cols], in_=grouped[:])
+
+        for i in range(TILES):
+            quantize_g(i, gather_and_turn(g_rows[i]))
+
+        whole = slice(0, N)
+        halves = [slice(0, N // 2), slice(N // 2, N)]
+        acc0 = multiply(0, gather_and_turn(x_rows[0]))
+        gate0 = agree(0, acc0, whole)
+        grouped1 = gather_and_turn(x_rows[1])
+        finish(0, acc0, whole, gate0)
+        acc1 = multiply(1, grouped1)
+        grouped2 = gather_and_turn(x_rows[2])
+        gate1 = agree(1, acc1, whole)
+        acc2 = multiply(2, grouped2)
+        finish(1, acc1, whole, gate1)
+        grouped3 = gather_and_turn(x_rows[3])
+        gate2 = agree(2, acc2, whole)
+        acc3 = multiply(3, grouped3)
+        finish(2, acc2, whole, gate2)
+        gates = [agree(3, acc3, cols) for cols in halves]
+        for cols, gate in zip(halves, gates):
+            finish(3, acc3, cols, gate)

@@ -19,63 +19,81 @@ SIGMOID = mybir.ActivationFunctionType.Sigmoid
 P = 128
 TILES = 4
 STEP = 0.04
+ROW_BYTES = 4 * T
 
 
 def tile_list_agreeing_update_kernel(tc, xt, g, mom, offs, out):
     nc = tc.nc
     with ExitStack() as ctx:
         keep = ctx.enter_context(tc.tile_pool(name="keep", bufs=1))
-        ring = ctx.enter_context(tc.tile_pool(name="ring", bufs=3))
+        placed = ctx.enter_context(tc.tile_pool(name="placed", bufs=1))
+        ring = ctx.enter_context(tc.tile_pool(name="ring", bufs=4))
         turn_psum = ctx.enter_context(tc.psum_pool(name="turn_psum", bufs=3))
         acc_psum = ctx.enter_context(tc.psum_pool(name="acc_psum", bufs=4))
 
         offsets = keep.tile([P, J // 16], U16, name="offsets")
         g_rows = [keep.tile([P, T], F32, name="g_rows%d" % i) for i in range(TILES)]
-        x_rows = [keep.tile([P, T], F32, name="x_rows%d" % i) for i in range(TILES)]
-        mom_pair = [keep.tile([P, 2, N], F32, name="mom_pair%d" % h) for h in range(2)]
-        x_view = xt.rearrange("(p i) t -> p i t", i=TILES)
-        mom_view = mom.rearrange("(p i) n -> p i n", i=TILES)
-        out_view = out.rearrange("(p i) n -> p i n", i=TILES)
+        x_rows = [placed.tile([P, T], F32, name="x_rows%d" % i, offset=i * ROW_BYTES, align_bytes=64) for i in range(TILES)]
+        mom_rows = [keep.tile([P, N], F32, name="mom_rows%d" % i) for i in range(TILES)]
 
-        nc.sync.dma_start(out=g_rows[0][:], in_=g[0:P, :])
+        def load_g(i):
+            nc.sync.dma_start(out=g_rows[i][:], in_=g[i * P:(i + 1) * P, :])
+
+        def load_x(i):
+            nc.sync.dma_start(out=x_rows[i][:], in_=xt[i * P:(i + 1) * P, :])
+
+        def load_mom(i):
+            nc.sync.dma_start(out=mom_rows[i][:], in_=mom[i * P:(i + 1) * P, :])
+
+        load_g(0)
         nc.sync.dma_start(offsets[:], offs)
         for i in range(1, TILES):
-            nc.sync.dma_start(out=g_rows[i][:], in_=g[i * P:(i + 1) * P, :])
-        nc.sync.dma_start(out=x_rows[0][:], in_=x_view[:, 0, :])
-        nc.sync.dma_start(out=mom_pair[0][:], in_=mom_view[:, 0:2, :])
+            load_g(i)
+        load_x(0)
+        load_mom(0)
         for i in range(1, TILES):
-            nc.sync.dma_start(out=x_rows[i][:], in_=x_view[:, i, :])
-        nc.sync.dma_start(out=mom_pair[1][:], in_=mom_view[:, 2:4, :])
+            load_x(i)
+        for i in range(1, TILES):
+            load_mom(i)
 
         ident = keep.tile([P, P], F32, name="ident")
         make_identity(nc, ident[:])
 
-        g_codes = keep.tile([P, N], U32, name="g_codes", align_bytes=64)
-        g_scales = keep.tile([P, N], U8, name="g_scales", align_bytes=64)
-        x_codes = [keep.tile([P, P], U32, name="x_codes%d" % i, align_bytes=64) for i in range(TILES)]
-        x_scales = [keep.tile([P, P], U8, name="x_scales%d" % i, align_bytes=64) for i in range(TILES)]
+        def new_tile(name, width, dtype, behind, at):
+            if behind is None:
+                return keep.tile([P, width], dtype, name=name, align_bytes=64)
+            return placed.tile([P, width], dtype, name=name, offset=behind * ROW_BYTES + at, align_bytes=64)
 
-        def gather_and_turn(rows):
+        g_grouped = keep.tile([P, 4 * N], BF16, name="g_grouped", align_bytes=64)
+
+        def gather_and_turn(rows, grouped):
             picked = ring.tile([P, J], BF16, name="picked", align_bytes=64)
-            nc.vector.tensor_copy(picked[:], rows[:].indirect(offsets[:]))
+            nc.vector.tensor_copy(
+                picked[:].rearrange("p (u b x) -> p b u x", u=2, b=16), rows[:].indirect(offsets[:])
+            )
             words = picked[:].bitcast(F32)
             turned = turn_psum.tile([P, 2, P], F32, name="turned")
             for u in range(2):
-                nc.tensor.transpose(turned[:, u, :], words[:, u:J // 2:2], ident[:])
-            grouped = ring.tile([P, 4 * P], BF16, name="grouped", align_bytes=64)
+                nc.tensor.transpose(turned[:, u, :], words[:, u * P:(u + 1) * P], ident[:])
             nc.scalar.copy(
-                out=grouped[:].bitcast(F32).rearrange("p (r u) -> p r u", u=2),
+                out=grouped.bitcast(F32).rearrange("p (r u) -> p r u", u=2),
                 in_=turned[:].rearrange("p u r -> p r u"),
             )
+
+        def gather_x(i):
+            grouped = placed.tile([P, 4 * P], BF16, name="grouped%d" % i, offset=(TILES + i) * ROW_BYTES + 2048, align_bytes=64)
+            gather_and_turn(x_rows[i], grouped[:])
             return grouped
 
-        def multiply(i, grouped):
-            nc.vector.quantize_mx(out=x_codes[i][:].bitcast(E4M3), scales=x_scales[i][:], in_=grouped[:])
+        def multiply(i, grouped, g_codes, g_scales, behind):
+            x_codes = new_tile("x_codes%d" % i, P, U32, behind, 0)
+            x_scales = new_tile("x_scales%d" % i, P, U8, None, 0)
+            nc.vector.quantize_mx(out=x_codes[:].bitcast(E4M3), scales=x_scales[:], in_=grouped[:])
             acc = acc_psum.tile([P, N], F32, name="acc")
             nc.tensor.matmul_mx(
                 out=acc[:],
-                lhsT=x_codes[i][:].bitcast(E4M3),
-                lhsT_scale=x_scales[i][:],
+                lhsT=x_codes[:].bitcast(E4M3),
+                lhsT_scale=x_scales[:],
                 rhs=g_codes[:].bitcast(E5M2),
                 rhs_scale=g_scales[:],
                 start=True,
@@ -83,42 +101,45 @@ def tile_list_agreeing_update_kernel(tc, xt, g, mom, offs, out):
             )
             return acc
 
-        def agree(i, acc, cols):
+        def agree(i, acc, cols, behind):
             width = cols.stop - cols.start
-            agreement = ring.tile([P, width], F32, name="agreement")
-            nc.vector.tensor_tensor(agreement[:], acc[:, cols], mom_pair[i // 2][:, i % 2, cols], MULT)
+            agreement = new_tile("agreement%d_%d" % (i, cols.start), width, F32, behind, 2048)
+            nc.vector.tensor_tensor(agreement[:], acc[:, cols], mom_rows[i][:, cols], MULT)
             gate = ring.tile([P, width], F32, name="gate")
             nc.scalar.activation(gate[:], agreement[:], SIGMOID, scale=2.0 * STEP)
             return gate
 
-        def finish(i, acc, cols, gate):
+        def finish(i, acc, cols, gate, behind):
             width = cols.stop - cols.start
-            result = ring.tile([P, width], F32, name="result")
+            result = new_tile("result%d_%d" % (i, cols.start), width, F32, behind, 4096)
             nc.vector.scalar_tensor_tensor(result[:], acc[:, cols], STEP, gate[:], MULT, MULT)
-            nc.sync.dma_start(out=out_view[:, i, cols], in_=result[:])
+            nc.sync.dma_start(out=out[i * P:(i + 1) * P, cols], in_=result[:])
 
-        def quantize_g(i, grouped):
-            cols = slice(i * P, (i + 1) * P)
-            nc.vector.quantize_mx(out=g_codes[:, cols].bitcast(E5M2), scales=g_scales[:, cols], in_=grouped[:])
+        warm = keep.tile([P, 1], F32, name="warm")
+        nc.scalar.activation(warm[:], ident[:, 0:1], SIGMOID, scale=2.0 * STEP)
 
         for i in range(TILES):
-            quantize_g(i, gather_and_turn(g_rows[i]))
+            gather_and_turn(g_rows[i], g_grouped[:, i * 4 * P:(i + 1) * 4 * P])
 
         whole = slice(0, N)
         halves = [slice(0, N // 2), slice(N // 2, N)]
-        acc0 = multiply(0, gather_and_turn(x_rows[0]))
-        gate0 = agree(0, acc0, whole)
-        grouped1 = gather_and_turn(x_rows[1])
-        finish(0, acc0, whole, gate0)
-        acc1 = multiply(1, grouped1)
-        grouped2 = gather_and_turn(x_rows[2])
-        gate1 = agree(1, acc1, whole)
-        acc2 = multiply(2, grouped2)
-        finish(1, acc1, whole, gate1)
-        grouped3 = gather_and_turn(x_rows[3])
-        gate2 = agree(2, acc2, whole)
-        acc3 = multiply(3, grouped3)
-        finish(2, acc2, whole, gate2)
-        gates = [agree(3, acc3, cols) for cols in halves]
+        grouped0 = gather_x(0)
+        g_codes = new_tile("g_codes", N, U32, 0, 0)
+        g_scales = new_tile("g_scales", N, U8, None, 0)
+        nc.vector.quantize_mx(out=g_codes[:].bitcast(E5M2), scales=g_scales[:], in_=g_grouped[:])
+        acc0 = multiply(0, grouped0, g_codes, g_scales, None)
+        grouped1 = gather_x(1)
+        gate0 = agree(0, acc0, whole, 1)
+        grouped2 = gather_x(2)
+        acc1 = multiply(1, grouped1, g_codes, g_scales, 2)
+        finish(0, acc0, whole, gate0, 2)
+        grouped3 = gather_x(3)
+        acc2 = multiply(2, grouped2, g_codes, g_scales, 3)
+        gate1 = agree(1, acc1, whole, 3)
+        acc3 = multiply(3, grouped3, g_codes, g_scales, None)
+        gate2 = agree(2, acc2, whole, TILES + 3)
+        finish(1, acc1, whole, gate1, None)
+        gates = [agree(3, acc3, cols, None) for cols in halves]
+        finish(2, acc2, whole, gate2, None)
         for cols, gate in zip(halves, gates):
-            finish(3, acc3, cols, gate)
+            finish(3, acc3, cols, gate, None)

@@ -14,6 +14,7 @@ U8 = mybir.dt.uint8
 E4M3 = mybir.dt.float8_e4m3fn_x4
 E5M2 = mybir.dt.float8_e5m2_x4
 MULT = mybir.AluOpType.mult
+COPY = mybir.ActivationFunctionType.Copy
 SIGMOID = mybir.ActivationFunctionType.Sigmoid
 
 P = 128
@@ -27,7 +28,7 @@ def tile_list_agreeing_update_kernel(tc, xt, g, mom, offs, out):
     with ExitStack() as ctx:
         keep = ctx.enter_context(tc.tile_pool(name="keep", bufs=1))
         placed = ctx.enter_context(tc.tile_pool(name="placed", bufs=1))
-        ring = ctx.enter_context(tc.tile_pool(name="ring", bufs=4))
+        ring = ctx.enter_context(tc.tile_pool(name="ring", bufs=6))
         turn_psum = ctx.enter_context(tc.psum_pool(name="turn_psum", bufs=3))
         acc_psum = ctx.enter_context(tc.psum_pool(name="acc_psum", bufs=4))
 
@@ -49,10 +50,10 @@ def tile_list_agreeing_update_kernel(tc, xt, g, mom, offs, out):
         nc.sync.dma_start(offsets[:], offs)
         for i in range(1, TILES):
             load_g(i)
-        load_x(0)
-        load_mom(0)
-        for i in range(1, TILES):
+        for i in range(TILES - 1):
             load_x(i)
+        load_mom(0)
+        load_x(3)
         for i in range(1, TILES):
             load_mom(i)
 
@@ -103,7 +104,7 @@ def tile_list_agreeing_update_kernel(tc, xt, g, mom, offs, out):
 
         def agree(i, acc, cols, behind):
             width = cols.stop - cols.start
-            agreement = new_tile("agreement%d_%d" % (i, cols.start), width, F32, behind, 2048)
+            agreement = new_tile("agreement%d_%d" % (i, cols.start), width, F32, behind, 512)
             nc.vector.tensor_tensor(agreement[:], acc[:, cols], mom_rows[i][:, cols], MULT)
             gate = ring.tile([P, width], F32, name="gate")
             nc.scalar.activation(gate[:], agreement[:], SIGMOID, scale=2.0 * STEP)
@@ -115,6 +116,17 @@ def tile_list_agreeing_update_kernel(tc, xt, g, mom, offs, out):
             nc.vector.scalar_tensor_tensor(result[:], acc[:, cols], STEP, gate[:], MULT, MULT)
             nc.sync.dma_start(out=out[i * P:(i + 1) * P, cols], in_=result[:])
 
+        def scaled_copy(i, acc):
+            w = keep.tile([P, N], F32, name="w%d" % i)
+            nc.scalar.activation(w[:], acc[:], COPY, scale=STEP)
+            return w
+
+        def finish_on_gpsimd(i, w, cols, gate, behind, at):
+            width = cols.stop - cols.start
+            result = new_tile("result%d_%d" % (i, cols.start), width, F32, behind, at)
+            nc.gpsimd.tensor_tensor(result[:], w[:, cols], gate[:, cols], MULT)
+            nc.sync.dma_start(out=out[i * P:(i + 1) * P, cols], in_=result[:])
+
         warm = keep.tile([P, 1], F32, name="warm")
         nc.scalar.activation(warm[:], ident[:, 0:1], SIGMOID, scale=2.0 * STEP)
 
@@ -122,24 +134,26 @@ def tile_list_agreeing_update_kernel(tc, xt, g, mom, offs, out):
             gather_and_turn(g_rows[i], g_grouped[:, i * 4 * P:(i + 1) * 4 * P])
 
         whole = slice(0, N)
-        halves = [slice(0, N // 2), slice(N // 2, N)]
+        halves = [slice(0, 192), slice(192, 384), slice(384, N)]
         grouped0 = gather_x(0)
         g_codes = new_tile("g_codes", N, U32, 0, 0)
         g_scales = new_tile("g_scales", N, U8, None, 0)
         nc.vector.quantize_mx(out=g_codes[:].bitcast(E5M2), scales=g_scales[:], in_=g_grouped[:])
-        acc0 = multiply(0, grouped0, g_codes, g_scales, None)
         grouped1 = gather_x(1)
-        gate0 = agree(0, acc0, whole, 1)
+        acc0 = multiply(0, grouped0, g_codes, g_scales, 1)
+        w0 = scaled_copy(0, acc0)
         grouped2 = gather_x(2)
         acc1 = multiply(1, grouped1, g_codes, g_scales, 2)
-        finish(0, acc0, whole, gate0, 2)
+        gate0 = agree(0, acc0, whole, 2)
+        acc2 = multiply(2, grouped2, g_codes, g_scales, None)
+        w2 = scaled_copy(2, acc2)
         grouped3 = gather_x(3)
-        acc2 = multiply(2, grouped2, g_codes, g_scales, 3)
+        finish_on_gpsimd(0, w0, whole, gate0, 3, 4096)
         gate1 = agree(1, acc1, whole, 3)
+        gate2 = agree(2, acc2, whole, None)
         acc3 = multiply(3, grouped3, g_codes, g_scales, None)
-        gate2 = agree(2, acc2, whole, TILES + 3)
         finish(1, acc1, whole, gate1, None)
+        finish_on_gpsimd(2, w2, whole, gate2, None, 0)
         gates = [agree(3, acc3, cols, None) for cols in halves]
-        finish(2, acc2, whole, gate2, None)
         for cols, gate in zip(halves, gates):
             finish(3, acc3, cols, gate, None)

@@ -30,15 +30,15 @@ def tile_list_agreeing_update_kernel(tc, xt, g, mom, offs, out):
         placed = ctx.enter_context(tc.tile_pool(name="placed", bufs=1))
         ring = ctx.enter_context(tc.tile_pool(name="ring", bufs=6))
         turn_psum = ctx.enter_context(tc.psum_pool(name="turn_psum", bufs=3))
-        acc_psum = ctx.enter_context(tc.psum_pool(name="acc_psum", bufs=4))
+        acc_psum = ctx.enter_context(tc.psum_pool(name="acc_psum", bufs=5))
 
         offsets = keep.tile([P, J // 16], U16, name="offsets")
-        g_rows = [keep.tile([P, T], F32, name="g_rows%d" % i) for i in range(TILES)]
+        g_rows = [keep.tile([P, 2 * T], F32, name="g_rows%d" % h) for h in range(2)]
         x_rows = [placed.tile([P, T], F32, name="x_rows%d" % i, offset=i * ROW_BYTES, align_bytes=64) for i in range(TILES)]
         mom_rows = [keep.tile([P, N], F32, name="mom_rows%d" % i) for i in range(TILES)]
 
         def load_g(i):
-            nc.sync.dma_start(out=g_rows[i][:], in_=g[i * P:(i + 1) * P, :])
+            nc.sync.dma_start(out=g_rows[i][:], in_=g[2 * i * P:2 * (i + 1) * P, :].rearrange("(p e) t -> p (e t)", e=2))
 
         def load_x(i):
             nc.sync.dma_start(out=x_rows[i][:], in_=xt[i * P:(i + 1) * P, :])
@@ -48,8 +48,7 @@ def tile_list_agreeing_update_kernel(tc, xt, g, mom, offs, out):
 
         load_g(0)
         nc.sync.dma_start(offsets[:], offs)
-        for i in range(1, TILES):
-            load_g(i)
+        load_g(1)
         for i in range(TILES - 1):
             load_x(i)
         load_mom(0)
@@ -90,17 +89,20 @@ def tile_list_agreeing_update_kernel(tc, xt, g, mom, offs, out):
             x_codes = new_tile("x_codes%d" % i, P, U32, behind, 0)
             x_scales = new_tile("x_scales%d" % i, P, U8, None, 0)
             nc.vector.quantize_mx(out=x_codes[:].bitcast(E4M3), scales=x_scales[:], in_=grouped[:])
-            acc = acc_psum.tile([P, N], F32, name="acc")
-            nc.tensor.matmul_mx(
-                out=acc[:],
-                lhsT=x_codes[:].bitcast(E4M3),
-                lhsT_scale=x_scales[:],
-                rhs=g_codes[:].bitcast(E5M2),
-                rhs_scale=g_scales[:],
-                start=True,
-                stop=True,
-            )
-            return acc
+            accs = []
+            for r in range(2 if i == 2 else 1):
+                acc = acc_psum.tile([P, N], F32, name="acc")
+                nc.tensor.matmul_mx(
+                    out=acc[:],
+                    lhsT=x_codes[:].bitcast(E4M3),
+                    lhsT_scale=x_scales[:],
+                    rhs=g_codes[:].bitcast(E5M2),
+                    rhs_scale=g_scales[:],
+                    start=True,
+                    stop=True,
+                )
+                accs.append(acc)
+            return accs if i == 2 else acc
 
         def agree(i, acc, cols, behind):
             width = cols.stop - cols.start
@@ -130,8 +132,26 @@ def tile_list_agreeing_update_kernel(tc, xt, g, mom, offs, out):
         warm = keep.tile([P, 1], F32, name="warm")
         nc.scalar.activation(warm[:], ident[:, 0:1], SIGMOID, scale=2.0 * STEP)
 
-        for i in range(TILES):
-            gather_and_turn(g_rows[i], g_grouped[:, i * 4 * P:(i + 1) * 4 * P])
+        def gate_part(agreement, cols):
+            gate = ring.tile([P, N], F32, name="gate")
+            nc.scalar.activation(gate[:, cols], agreement[:, cols], SIGMOID, scale=2.0 * STEP)
+            return gate
+
+        for h in range(2):
+            turned = turn_psum.tile([P, 4, P], F32, name="turned")
+            for e in range(2):
+                picked = ring.tile([P, J], BF16, name="picked", align_bytes=64)
+                nc.vector.tensor_copy(
+                    picked[:].rearrange("p (u b x) -> p b u x", u=2, b=16),
+                    g_rows[h][:, e * T:(e + 1) * T].indirect(offsets[:]),
+                )
+                words = picked[:].bitcast(F32)
+                for u in range(2):
+                    nc.tensor.transpose(turned[:, 2 * e + u, :], words[:, u * P:(u + 1) * P], ident[:])
+            nc.scalar.copy(
+                out=g_grouped[:, h * 8 * P:(h + 1) * 8 * P].bitcast(F32).rearrange("p (r v) -> p r v", v=4),
+                in_=turned[:].rearrange("p v r -> p r v"),
+            )
 
         whole = slice(0, N)
         halves = [slice(0, 192), slice(192, 384), slice(384, N)]
@@ -145,15 +165,19 @@ def tile_list_agreeing_update_kernel(tc, xt, g, mom, offs, out):
         grouped2 = gather_x(2)
         acc1 = multiply(1, grouped1, g_codes, g_scales, 2)
         gate0 = agree(0, acc0, whole, 2)
-        acc2 = multiply(2, grouped2, g_codes, g_scales, None)
-        w2 = scaled_copy(2, acc2)
+        acc2, twin2 = multiply(2, grouped2, g_codes, g_scales, None)
+        w2 = scaled_copy(2, twin2)
         grouped3 = gather_x(3)
         finish_on_gpsimd(0, w0, whole, gate0, 3, 4096)
         gate1 = agree(1, acc1, whole, 3)
-        gate2 = agree(2, acc2, whole, None)
+        agreement2 = keep.tile([P, N], F32, name="agreement2")
+        nc.vector.tensor_tensor(agreement2[:], acc2[:], mom_rows[2][:], MULT)
+        sides = [slice(0, N // 2), slice(N // 2, N)]
+        gates2 = [gate_part(agreement2, cols) for cols in sides]
         acc3 = multiply(3, grouped3, g_codes, g_scales, None)
         finish(1, acc1, whole, gate1, None)
-        finish_on_gpsimd(2, w2, whole, gate2, None, 0)
+        for cols, gate in zip(sides, gates2):
+            finish_on_gpsimd(2, w2, cols, gate, None, 0)
         gates = [agree(3, acc3, cols, None) for cols in halves]
         for cols, gate in zip(halves, gates):
             finish(3, acc3, cols, gate, None)

from contextlib import ExitStack

import concourse.mybir as mybir
from concourse.masks import make_identity

K, N, T, J = 512, 512, 2048, 512
FLOPS = 2 * K * N * J

F32 = mybir.dt.float32
BF16 = mybir.dt.bfloat16
U32 = mybir.dt.uint32
U16 = mybir.dt.uint16
U8 = mybir.dt.uint8
E4M3 = mybir.dt.float8_e4m3fn_x4
E5M2 = mybir.dt.float8_e5m2_x4
MULT = mybir.AluOpType.mult
COPY = mybir.ActivationFunctionType.Copy
SIGMOID = mybir.ActivationFunctionType.Sigmoid

P = 128
TILES = 4
STEP = 0.04
ROW_BYTES = 4 * T


def tile_list_agreeing_update_kernel(tc, xt, g, mom, offs, out):
    nc = tc.nc
    with ExitStack() as ctx:
        keep = ctx.enter_context(tc.tile_pool(name="keep", bufs=1))
        placed = ctx.enter_context(tc.tile_pool(name="placed", bufs=1))
        ring = ctx.enter_context(tc.tile_pool(name="ring", bufs=6))
        turn_psum = ctx.enter_context(tc.psum_pool(name="turn_psum", bufs=3))
        acc_psum = ctx.enter_context(tc.psum_pool(name="acc_psum", bufs=5))

        offsets = keep.tile([P, J // 16], U16, name="offsets")
        g_rows = [keep.tile([P, 2 * T], F32, name="g_rows%d" % h) for h in range(2)]
        x_rows = [placed.tile([P, T], F32, name="x_rows%d" % i, offset=i * ROW_BYTES, align_bytes=64) for i in range(TILES)]
        mom_rows = [keep.tile([P, N], F32, name="mom_rows%d" % i) for i in range(TILES)]

        def load_g(i):
            nc.sync.dma_start(out=g_rows[i][:], in_=g[2 * i * P:2 * (i + 1) * P, :].rearrange("(p e) t -> p (e t)", e=2))

        def load_x(i):
            nc.sync.dma_start(out=x_rows[i][:], in_=xt[i * P:(i + 1) * P, :])

        def load_mom(i):
            nc.sync.dma_start(out=mom_rows[i][:], in_=mom[i * P:(i + 1) * P, :])

        load_g(0)
        nc.sync.dma_start(offsets[:], offs)
        load_g(1)
        for i in range(TILES - 1):
            load_x(i)
        load_mom(0)
        load_x(3)
        for i in range(1, TILES):
            load_mom(i)

        ident = keep.tile([P, P], F32, name="ident")
        make_identity(nc, ident[:])

        def new_tile(name, width, dtype, behind, at):
            if behind is None:
                return keep.tile([P, width], dtype, name=name, align_bytes=64)
            return placed.tile([P, width], dtype, name=name, offset=behind * ROW_BYTES + at, align_bytes=64)

        g_grouped = keep.tile([P, 4 * N], BF16, name="g_grouped", align_bytes=64)

        def gather_and_turn(rows, grouped):
            picked = ring.tile([P, J], BF16, name="picked", align_bytes=64)
            nc.vector.tensor_copy(
                picked[:].rearrange("p (u b x) -> p b u x", u=2, b=16), rows[:].indirect(offsets[:])
            )
            words = picked[:].bitcast(F32)
            turned = turn_psum.tile([P, 2, P], F32, name="turned")
            for u in range(2):
                nc.tensor.transpose(turned[:, u, :], words[:, u * P:(u + 1) * P], ident[:])
            nc.scalar.copy(
                out=grouped.bitcast(F32).rearrange("p (r u) -> p r u", u=2),
                in_=turned[:].rearrange("p u r -> p r u"),
            )

        def gather_x(i):
            grouped = placed.tile([P, 4 * P], BF16, name="grouped%d" % i, offset=(TILES + i) * ROW_BYTES + 2048, align_bytes=64)
            gather_and_turn(x_rows[i], grouped[:])
            return grouped

        def multiply(i, grouped, g_codes, g_scales, behind):
            x_codes = new_tile("x_codes%d" % i, P, U32, behind, 0)
            x_scales = new_tile("x_scales%d" % i, P, U8, None, 0)
            nc.vector.quantize_mx(out=x_codes[:].bitcast(E4M3), scales=x_scales[:], in_=grouped[:])
            accs = []
            for r in range(2 if i == 2 else 1):
                acc = acc_psum.tile([P, N], F32, name="acc")
                nc.tensor.matmul_mx(
                    out=acc[:],
                    lhsT=x_codes[:].bitcast(E4M3),
                    lhsT_scale=x_scales[:],
                    rhs=g_codes[:].bitcast(E5M2),
                    rhs_scale=g_scales[:],
                    start=True,
                    stop=True,
                )
                accs.append(acc)
            return accs if i == 2 else acc

        def agree(i, acc, cols, behind):
            width = cols.stop - cols.start
            agreement = new_tile("agreement%d_%d" % (i, cols.start), width, F32, behind, 512)
            nc.vector.tensor_tensor(agreement[:], acc[:, cols], mom_rows[i][:, cols], MULT)
            gate = ring.tile([P, width], F32, name="gate")
            nc.scalar.activation(gate[:], agreement[:], SIGMOID, scale=2.0 * STEP)
            return gate

        def finish(i, acc, cols, gate, behind):
            width = cols.stop - cols.start
            result = new_tile("result%d_%d" % (i, cols.start), width, F32, behind, 4096)
            nc.vector.scalar_tensor_tensor(result[:], acc[:, cols], STEP, gate[:], MULT, MULT)
            nc.sync.dma_start(out=out[i * P:(i + 1) * P, cols], in_=result[:])

        def scaled_copy(i, acc):
            w = keep.tile([P, N], F32, name="w%d" % i)
            nc.scalar.activation(w[:], acc[:], COPY, scale=STEP)
            return w

        def finish_on_gpsimd(i, w, cols, gate, behind, at):
            width = cols.stop - cols.start
            result = new_tile("result%d_%d" % (i, cols.start), width, F32, behind, at)
            nc.gpsimd.tensor_tensor(result[:], w[:, cols], gate[:, cols], MULT)
            nc.sync.dma_start(out=out[i * P:(i + 1) * P, cols], in_=result[:])

        warm = keep.tile([P, 1], F32, name="warm")
        nc.scalar.activation(warm[:], ident[:, 0:1], SIGMOID, scale=2.0 * STEP)

        def gate_part(agreement, cols):
            gate = ring.tile([P, N], F32, name="gate")
            nc.scalar.activation(gate[:, cols], agreement[:, cols], SIGMOID, scale=2.0 * STEP)
            return gate

        for h in range(2):
            turned = turn_psum.tile([P, 4, P], F32, name="turned")
            for e in range(2):
                picked = ring.tile([P, J], BF16, name="picked", align_bytes=64)
                nc.vector.tensor_copy(
                    picked[:].rearrange("p (u b x) -> p b u x", u=2, b=16),
                    g_rows[h][:, e * T:(e + 1) * T].indirect(offsets[:]),
                )
                words = picked[:].bitcast(F32)
                for u in range(2):
                    nc.tensor.transpose(turned[:, 2 * e + u, :], words[:, u * P:(u + 1) * P], ident[:])
            nc.scalar.copy(
                out=g_grouped[:, h * 8 * P:(h + 1) * 8 * P].bitcast(F32).rearrange("p (r v) -> p r v", v=4),
                in_=turned[:].rearrange("p v r -> p r v"),
            )

        whole = slice(0, N)
        halves = [slice(0, 192), slice(192, 384), slice(384, N)]
        grouped0 = gather_x(0)
        g_codes = new_tile("g_codes", N, U32, 0, 0)
        g_scales = new_tile("g_scales", N, U8, None, 0)
        nc.vector.quantize_mx(out=g_codes[:].bitcast(E5M2), scales=g_scales[:], in_=g_grouped[:])
        grouped1 = gather_x(1)
        acc0 = multiply(0, grouped0, g_codes, g_scales, 1)
        w0 = scaled_copy(0, acc0)
        grouped2 = gather_x(2)
        acc1 = multiply(1, grouped1, g_codes, g_scales, 2)
        gate0 = agree(0, acc0, whole, 2)
        acc2, twin2 = multiply(2, grouped2, g_codes, g_scales, None)
        w2 = scaled_copy(2, twin2)
        grouped3 = gather_x(3)
        finish_on_gpsimd(0, w0, whole, gate0, 3, 4096)
        gate1 = agree(1, acc1, whole, 3)
        agreement2 = keep.tile([P, N], F32, name="agreement2")
        nc.vector.tensor_tensor(agreement2[:], acc2[:], mom_rows[2][:], MULT)
        sides = [slice(0, N // 2), slice(N // 2, N)]
        gates2 = [gate_part(agreement2, cols) for cols in sides]
        acc3 = multiply(3, grouped3, g_codes, g_scales, None)
        finish(1, acc1, whole, gate1, None)
        for cols, gate in zip(sides, gates2):
            finish_on_gpsimd(2, w2, cols, gate, None, 0)
        gates = [agree(3, acc3, cols, None) for cols in halves]
        for cols, gate in zip(halves, gates):
            finish(3, acc3, cols, gate, None)
